import numpy as np
import ml_dtypes


def mxq(x, axis, fmt="e4m3"):
    dtype, down = {"e4m3": (ml_dtypes.float8_e4m3fn, 7), "e5m2": (ml_dtypes.float8_e5m2, 14)}[fmt]
    v = np.moveaxis(np.asarray(x, np.float32).astype(ml_dtypes.bfloat16).astype(np.float64), axis, -1)
    blocks = v.reshape(v.shape[:-1] + (-1, 32))
    amax = np.abs(blocks).max(-1, keepdims=True)
    byte = np.maximum(np.where(amax > 0, np.frexp(amax)[1] - 1 + 127, 0) - down, 1)
    scale = np.exp2(byte - 127.0)
    codes = (blocks / scale).astype(np.float32).astype(dtype).astype(np.float64)
    return np.moveaxis((codes * scale).reshape(v.shape), -1, axis)


WIDE = False


def mx_kscale(k):
    if not WIDE:
        return np.ones(k)
    levels = np.array([10, -10, 5, -5, 0])
    if k % 512:
        return np.exp2(np.random.permutation(np.resize(levels, k // 32))).repeat(32)
    a = np.empty((k // 512, 16))
    for p in range(k // 512):
        a[p, :8] = np.random.permutation(np.resize(levels, 8))
        for g in range(8):
            far = levels[np.abs(levels - a[p, g]) >= 10]
            a[p, g + 8] = far[np.random.randint(len(far))]
    return np.exp2(a.ravel()).repeat(32)


BF16 = ml_dtypes.bfloat16


def bf(x):
    return np.asarray(x, np.float32).astype(BF16)


def f64(x):
    return np.asarray(x).astype(np.float64)


E2M1 = np.array([0.0, 0.5, 1.0, 1.5, 2.0, 3.0, 4.0, 6.0, -0.0, -0.5, -1.0, -1.5, -2.0, -3.0, -4.0, -6.0])


def pack_weight(w, fmt):
    k, n = w.shape
    w = f64(bf(w)).reshape(k // 32, 32, n)
    amax = np.abs(w).max(1)
    if fmt == "e4m3":
        byte = np.frexp(amax)[1] - 1 + 127 - 7
    else:
        mant, ex = np.frexp(amax / 6.0)
        byte = np.where(mant > 0.5, ex, ex - 1) + 127
    byte = np.clip(np.where(amax > 0, byte, 1), 1, 254)
    scaled = (w * np.exp2(127.0 - byte)[:, None, :]).reshape(k, n).astype(np.float32)
    by_word = np.ascontiguousarray(scaled.reshape(k // 512, 128, 4, n).transpose(0, 1, 3, 2))
    if fmt == "e4m3":
        words = by_word.astype(ml_dtypes.float8_e4m3fn).view(np.uint8)
    else:
        c = by_word.astype(ml_dtypes.float4_e2m1fn).view(np.uint8) & 0xF
        words = c[..., 0::2] | (c[..., 1::2] << 4)
    return np.ascontiguousarray(words), np.ascontiguousarray(byte.astype(np.uint8).reshape(k // 512, 16, n))


def unpack_weight(words, scales, fmt):
    g, p, n, _ = words.shape
    if fmt == "e4m3":
        vals = np.ascontiguousarray(words).view(ml_dtypes.float8_e4m3fn).astype(np.float64)
    else:
        nib = np.empty((g, p, n, 4), np.uint8)
        nib[..., 0::2] = words & 0xF
        nib[..., 1::2] = words >> 4
        vals = E2M1[nib]
    vals = vals * np.repeat(np.exp2(scales.astype(np.float64) - 127.0), 8, axis=1)[..., None]
    return vals.transpose(0, 1, 3, 2).reshape(g * 512, n)
def pack4(w):
    words, scales = pack_weight(w, "e2m1")
    return words.reshape(words.shape[0], 128, -1), scales


def unpack4(words, scales):
    return unpack_weight(words.reshape(words.shape[0], 128, -1, 2), scales, "e2m1")


N, D, H, O = 1024, 1024, 1024, 512
DAMP = 0.2


def draw0():
    u = mx_kscale(O)
    t = mx_kscale(N)
    x = bf(np.random.standard_normal((N, D)))
    a = bf(np.random.standard_normal((N, H)))
    g = bf(np.random.standard_normal((N, O)) * u[None, :])
    w2 = np.random.standard_normal((H, O)) / np.sqrt(O) / u[None, :]
    w2_words, w2_scales = pack4(w2.T)
    return {
        "x": x,
        "a": a,
        "g": g,
        "w2_words": w2_words,
        "w2_scales": w2_scales,
        "p": bf(np.random.uniform(0.5, 1.5, N) * t),
        "q": bf(np.random.uniform(0.5, 1.5, N) / t),
        "s": bf(np.random.standard_normal(N)),
    }


def backprop_delta(a, g, w2_words, w2_scales):
    back = mxq(g, 1, "e4m3") @ unpack4(w2_words, w2_scales)
    return back * (1.0 - np.tanh(a) ** 2)


def core(x, a, g, w2_words, w2_scales, p, q, s):
    x, a, g, p, q, s = f64(x), f64(a), f64(g), f64(p), f64(q), f64(s)
    n = x.shape[0]

    d = backprop_delta(a, g, w2_words, w2_scales)

    xp = x * p[:, None]
    dq = d * q[:, None]
    grad = (mxq(xp, 0, "e4m3").T @ mxq(dq, 0, "e4m3")) / np.sqrt(n)

    x2 = x * xp * s[:, None]
    d2 = d * dq * s[:, None]
    fisher = (mxq(x2, 0, "e4m3").T @ mxq(d2, 0, "e4m3")) / n

    return grad / (fisher + DAMP)


def e4m3fn_bytes(y):
    return np.clip(np.asarray(y, np.float64), -448.0, 448.0).astype(np.float32).astype(ml_dtypes.float8_e4m3fn).view(np.uint8)


def e4m3fn_values(b):
    return np.asarray(b, np.uint8).view(ml_dtypes.float8_e4m3fn).astype(np.float64)


def setup_inputs():
    d = draw0()
    x0 = np.asarray(d['g']).astype(np.float64)
    s = (np.max(np.abs(x0), axis=(0,), keepdims=True) / 448.0).astype(np.float32)
    out = {}
    for k, v in d.items():
        if k == 'g':
            out['g_bytes'] = e4m3fn_bytes(x0 / s.astype(np.float64))
            out['g_scale'] = s
        else:
            out[k] = v
    return out


def reference(x, a, g_bytes, g_scale, w2_words, w2_scales, p, q, s):
    return core(x, a, e4m3fn_values(g_bytes) * g_scale.astype(np.float64), w2_words, w2_scales, p, q, s)

@@ -1,0 +1,381 @@
+from contextlib import ExitStack
+
+import concourse.mybir as mybir
+from concourse.masks import make_identity
+
+N, D, H, O = 1024, 1024, 1024, 512
+DAMP = 0.2
+FLOPS = 2 * N * D * H * 2 + 2 * N * O * H
+
+F32 = mybir.dt.float32
+BF16 = mybir.dt.bfloat16
+U32 = mybir.dt.uint32
+I32 = mybir.dt.int32
+U8 = mybir.dt.uint8
+FP8 = mybir.dt.float8_e4m3fn
+FP8X4 = mybir.dt.float8_e4m3fn_x4
+FP4X4 = mybir.dt.float4_e2m1fn_x4
+ACT = mybir.ActivationFunctionType
+ALU = mybir.AluOpType
+
+P = 128
+T = 4
+G = 2
+HB = 512
+UNITS = [(0, 0), (0, 1), (1, 0), (1, 1)]
+CHUNKS = [256, 256, 256, 128, 128]
+
+
+def tile_diagonalfishernaturalgradient_w4_kernel(tc, x, a, g_bytes, g_scale, w2_words, w2_scales, p, q, s, out):
+    nc = tc.nc
+    with ExitStack() as ctx:
+        keep = ctx.enter_context(tc.tile_pool(name="keep", bufs=1))
+        work = ctx.enter_context(tc.tile_pool(name="work", bufs=2))
+        epi = ctx.enter_context(tc.tile_pool(name="epi", bufs=4))
+        psum = ctx.enter_context(tc.psum_pool(name="psum", bufs=8))
+
+        g_raw = keep.tile([P, G, T, O], U8, align_bytes=64)
+        g_sc = keep.tile([P, O], F32, align_bytes=64)
+        g_bf = keep.tile([P, G, T, O], BF16, align_bytes=64)
+        g_int = keep.tile([P, G * T * O], BF16, align_bytes=64)
+        g_codes = keep.tile([P, G * T * P], U32, align_bytes=64)
+        g_scales = keep.tile([P, G * T * P], U8, align_bytes=64)
+        w_sb = keep.tile([P, 2 * H], U8, align_bytes=64)
+        w_scl = keep.tile([P, H], U8, align_bytes=64)
+        a_sb = keep.tile([P, G, T, H], BF16, align_bytes=64)
+        x_sb = keep.tile([P, G, T, D], BF16, align_bytes=64)
+        xp_pl = keep.tile([P, G, T, D], BF16, align_bytes=64)
+        v = keep.tile([P, G, 2, T, HB], F32, align_bytes=64)
+        dq_codes = keep.tile([P, G, H], U32, align_bytes=64)
+        dq_scales = keep.tile([P, G, H], U8, align_bytes=64)
+        d2_codes = keep.tile([P, G, H], U32, align_bytes=64)
+        d2_scales = keep.tile([P, G, H], U8, align_bytes=64)
+        p_sb = keep.tile([P, G * T], BF16)
+        q_sb = keep.tile([P, G * T], BF16)
+        s_sb = keep.tile([P, G * T], BF16)
+        s_abs = keep.tile([P, G * T], F32)
+        q_inv = keep.tile([P, G * T], F32)
+        sq_in = keep.tile([P, 3 * G * T], F32)
+        half = keep.tile([P, 3 * G * T], F32)
+        root = keep.tile([P, 3 * G * T], F32)
+        ident = keep.tile([P, P], F32)
+        warm = keep.tile([P, 1], F32)
+
+        with tc.manual_schedule():
+            x_v = x.rearrange("(g p t) d -> p g t d", g=G, t=T)
+            a_v = a.rearrange("(g p t) h -> p g t h", g=G, t=T)
+            g_v = g_bytes.rearrange("(g p t) o -> p g t o", g=G, t=T)
+            nc.gpsimd.memset(w_scl[:].bitcast(U32), 0)
+            nc.gpsimd.memset(half[:], 0.5)
+            make_identity(nc, ident[:])
+            nc.vector.memset(warm[:], 0.0)
+            nc.scalar.dma_start(out=g_sc[:], in_=g_scale.rearrange("o k -> (o k)").partition_broadcast(P))
+            nc.sync.dma_start(out=g_raw[:, 0], in_=g_v[:, 0])
+
+            def load_vector(dst, src):
+                nc.scalar.dma_start(out=dst[:].rearrange("p (g t) -> p g t", g=G), in_=src.rearrange("(g p t) -> p g t", g=G, t=T))
+
+            load_vector(q_sb, q)
+            load_vector(s_sb, s)
+            nc.scalar.activation(out=warm[:], in_=warm[:], func=ACT.Tanh)
+            for t in (0, 2):
+                nc.sync.dma_start(out=a_sb[:, 0, t : t + 2], in_=a_v[:, 0, t : t + 2])
+            nc.sync.dma_start(out=w_sb[:], in_=w2_words[0])
+            for quad in range(4):
+                nc.sync.dma_start(out=w_scl[32 * quad : 32 * quad + 4, :].bitcast(I32), in_=w2_scales[0, 4 * quad : 4 * quad + 4, :].bitcast(I32))
+            nc.sync.dma_start(out=p_sb[:].rearrange("p (g t) -> p g t", g=G), in_=p.rearrange("(g p t) -> p g t", g=G, t=T))
+            nc.sync.dma_start(out=g_raw[:, 1], in_=g_v[:, 1])
+            for t in (0, 2):
+                nc.sync.dma_start(out=a_sb[:, 1, t : t + 2], in_=a_v[:, 1, t : t + 2])
+            for g in range(G):
+                for t in (0, 2):
+                    nc.sync.dma_start(out=x_sb[:, g, t : t + 2], in_=x_v[:, g, t : t + 2])
+
+            def g_mul(g, t):
+                nc.vector.tensor_tensor(out=g_bf[:, g, t], in0=g_raw[:, g, t].bitcast(FP8), in1=g_sc[:], op=ALU.mult)
+
+            def g_turn(g, t0):
+                bank = psum.tile([P, HB], F32, name="bank")
+                for i in range(2):
+                    words = g_bf[:, g, t0 + i].bitcast(F32)
+                    for u in range(2):
+                        col = (2 * i + u) * P
+                        nc.tensor.transpose(bank[:, col : col + P], words[:, u : O // 2 : 2], ident[:])
+                return bank
+
+            def g_out(bank, g, t0):
+                base = (g * T + t0) * O
+                nc.scalar.copy(
+                    out=g_int[:, base : base + 2 * O].bitcast(F32).rearrange("p (i r u) -> p i r u", i=2, u=2),
+                    in_=bank[:].rearrange("p (i u r) -> p i r u", i=2, u=2),
+                )
+
+            def g_quant(g):
+                c0 = g * T * P
+                nc.vector.quantize_mx(
+                    out=g_codes[:, c0 : c0 + T * P].bitcast(FP8X4),
+                    scales=g_scales[:, c0 : c0 + T * P],
+                    in_=g_int[:, T * c0 : T * (c0 + T * P)],
+                )
+
+            def tanh(u, t0, n):
+                g, hb = u
+                nc.scalar.activation(out=v[:, g, hb, t0 : t0 + n], in_=a_sb[:, g, t0 : t0 + n, hb * HB : (hb + 1) * HB], func=ACT.Tanh)
+
+            def tanh_sq(u):
+                g, hb = u
+                for t in range(T):
+                    j = 2 * G * T + g * T + t
+                    nc.scalar.activation(out=v[:, g, hb, t], in_=v[:, g, hb, t], func=ACT.Square, scale=root[:, j : j + 1])
+
+            def back(u):
+                g, hb = u
+                banks = []
+                for t in range(T):
+                    bank = psum.tile([P, HB], F32, name="bank")
+                    c0 = (g * T + t) * P
+                    nc.tensor.matmul_mx(
+                        out=bank[:],
+                        lhsT=g_codes[:, c0 : c0 + P].bitcast(FP8X4),
+                        lhsT_scale=g_scales[:, c0 : c0 + P],
+                        rhs=w_sb[:, 2 * hb * HB : 2 * (hb + 1) * HB].bitcast(FP4X4),
+                        rhs_scale=w_scl[:, hb * HB : (hb + 1) * HB],
+                        start=True,
+                        stop=True,
+                    )
+                    banks.append(bank)
+                return banks
+
+            def v_mul(u, banks):
+                g, hb = u
+                for t in range(T):
+                    j = 2 * G * T + g * T + t
+                    nc.vector.scalar_tensor_tensor(
+                        out=v[:, g, hb, t], in0=v[:, g, hb, t], scalar=sq_in[:, j : j + 1], in1=banks[t][:], op0=ALU.subtract, op1=ALU.mult
+                    )
+
+            def d2_square(u):
+                g, hb = u
+                d2_pl = work.tile([P, T, HB], BF16, align_bytes=64, name="d2_pl")
+                for t in range(T):
+                    j = G * T + g * T + t
+                    nc.scalar.activation(out=d2_pl[:, t], in_=v[:, g, hb, t], func=ACT.Square, scale=root[:, j : j + 1])
+                return d2_pl
+
+            def interleave(dst, src):
+                nc.vector.tensor_copy(out=dst.rearrange("p (c i) t -> p c t i", i=4), in_=src.rearrange("p t (c i) -> p c t i", i=4))
+
+            def d_int(src, name):
+                dst = work.tile([P, HB, T], BF16, align_bytes=64, name=name)
+                interleave(dst[:], src)
+                return dst
+
+            def d_quant(u, src, codes, scales):
+                g, hb = u
+                cols = slice(hb * HB, (hb + 1) * HB)
+                nc.vector.quantize_mx(out=codes[:, g, cols].bitcast(FP8X4), scales=scales[:, g, cols], in_=src[:].rearrange("p n t -> p (n t)"))
+
+            nc.scalar.activation(out=s_abs[:], in_=s_sb[:], func=ACT.Abs)
+            qs = slice(2 * G * T, 3 * G * T)
+            nc.vector.tensor_scalar(out=sq_in[:, qs], in0=q_sb[:], scalar1=1e-30, scalar2=None, op0=ALU.max)
+            nc.vector.reciprocal(out=q_inv[:], in_=sq_in[:, qs])
+            nc.vector.tensor_tensor(out=sq_in[:, G * T : 2 * G * T], in0=q_inv[:], in1=s_abs[:], op=ALU.mult)
+            dsl = slice(G * T, 3 * G * T)
+            nc.gpsimd.tensor_tensor(out=root[:, dsl], in0=sq_in[:, dsl], in1=half[:, dsl], op=ALU.pow)
+
+            starts = [sum(CHUNKS[:i]) for i in range(len(CHUNKS))]
+
+            def xp_mul(half_no):
+                cols = slice(half_no * 512, (half_no + 1) * 512)
+                for g in range(G):
+                    for t in range(T):
+                        j = g * T + t
+                        nc.vector.tensor_scalar(out=xp_pl[:, g, t, cols], in0=x_sb[:, g, t, cols], scalar1=p_sb[:, j : j + 1], scalar2=None, op0=ALU.mult)
+
+            def x2_square(c):
+                d0, w = starts[c], CHUNKS[c]
+                x2_pl = work.tile([P, G, T, 256], BF16, align_bytes=64, name="x2_pl", bufs=3)
+
+                def one(g, t):
+                    j = g * T + t
+                    nc.scalar.activation(out=x2_pl[:, g, t, 0:w], in_=x_sb[:, g, t, d0 : d0 + w], func=ACT.Square, scale=root[:, j : j + 1])
+
+                return x2_pl, [lambda g=g, t=t: one(g, t) for g in range(G) for t in range(T)]
+
+            def x_int(src, w, name):
+                dst = work.tile([P, G, 256, T], BF16, align_bytes=64, name=name)
+                return dst, [lambda g=g: interleave(dst[:].rearrange("p g n t -> p (g n) t")[:, g * w : (g + 1) * w, :], src[:, g]) for g in range(G)]
+
+            def x_quant(src, w, name):
+                codes = work.tile([P, G * 256], U32, align_bytes=64, name=name + "_codes")
+                scales = work.tile([P, G * 256], U8, align_bytes=64, name=name + "_scales")
+                nc.vector.quantize_mx(
+                    out=codes[:, 0 : G * w].bitcast(FP8X4),
+                    scales=scales[:, 0 : G * w],
+                    in_=src[:].rearrange("p g n t -> p (g n t)")[:, 0 : G * w * T],
+                )
+                return codes, scales
+
+            def product(lhs, w, m, rhs_codes, rhs_scales, hb):
+                bank = psum.tile([P, HB], F32, name="bank")
+                codes, scales = lhs
+                for g in range(G):
+                    c0 = g * w + m * P
+                    nc.tensor.matmul_mx(
+                        out=bank[:],
+                        lhsT=codes[:, c0 : c0 + P].bitcast(FP8X4),
+                        lhsT_scale=scales[:, c0 : c0 + P],
+                        rhs=rhs_codes[:, g, hb * HB : (hb + 1) * HB].bitcast(FP8X4),
+                        rhs_scale=rhs_scales[:, g, hb * HB : (hb + 1) * HB],
+                        start=(g == 0),
+                        stop=(g == G - 1),
+                    )
+                return bank
+
+            def ars(fb):
+                r = epi.tile([P, HB], F32, name="r")
+                nc.scalar.activation(out=r[:], in_=fb[:], func=ACT.Abs_reciprocal_sqrt, scale=1.0 / N, bias=DAMP)
+                return r
+
+            def square_r(r):
+                r2 = epi.tile([P, HB], F32, name="r2")
+                nc.scalar.activation(out=r2[:], in_=r[:], func=ACT.Square)
+                return r2
+
+            def finish(gb, r2, d0, hb):
+                y = epi.tile([P, HB], F32, name="y")
+                nc.vector.scalar_tensor_tensor(out=y[:], in0=gb[:], scalar=-1.0 / 32.0, in1=r2[:], op0=ALU.mult, op1=ALU.mult)
+                nc.sync.dma_start(out=out[d0 : d0 + P, hb * HB : (hb + 1) * HB], in_=y[:])
+
+            def finish_twice(gb, r, d0, hb):
+                y = epi.tile([P, HB], F32, name="y")
+                nc.vector.scalar_tensor_tensor(out=y[:], in0=gb[:], scalar=-1.0 / 32.0, in1=r[:], op0=ALU.mult, op1=ALU.mult)
+                z = epi.tile([P, HB], F32, name="z")
+                nc.vector.tensor_tensor(out=z[:], in0=y[:], in1=r[:], op=ALU.mult)
+                nc.sync.dma_start(out=out[d0 : d0 + P, hb * HB : (hb + 1) * HB], in_=z[:])
+
+            x2_planes, x2_ops, x2_dst, xp_dst, x2_io, xp_io, x2_q, xp_q = {}, {}, {}, {}, {}, {}, {}, {}
+
+            def x2_start(c):
+                x2_planes[c], x2_ops[c] = x2_square(c)
+
+            def x_ints(c):
+                d0, w = starts[c], CHUNKS[c]
+                x2_dst[c], x2_io[c] = x_int(x2_planes[c][:, :, :, 0:w], w, "x2_int")
+                xp_dst[c], xp_io[c] = x_int(xp_pl[:, :, :, d0 : d0 + w], w, "xp_int")
+
+            def run(ops):
+                for op in ops:
+                    op()
+
+            for t in range(T):
+                g_mul(0, t)
+            tanh(UNITS[0], 0, 2)
+            g_out(g_turn(0, 0), 0, 0)
+            tanh(UNITS[0], 2, 2)
+            g_out(g_turn(0, 2), 0, 2)
+            g_quant(0)
+            tanh_sq(UNITS[0])
+            banks = back(UNITS[0])
+            d2_pl, dq_int, d2_int = {}, {}, {}
+            for i in range(4):
+                u = UNITS[i]
+                v_mul(u, banks)
+                if i == 0:
+                    for t in range(T):
+                        g_mul(1, t)
+                    turned = [g_turn(1, 0), g_turn(1, 2)]
+                if i + 1 < 4:
+                    tanh(UNITS[i + 1], 0, T)
+                    tanh_sq(UNITS[i + 1])
+                if i == 0:
+                    g_out(turned[0], 1, 0)
+                    g_out(turned[1], 1, 2)
+                d2_pl[i] = d2_square(u)
+                if i > 0:
+                    d2_int[i - 1] = d_int(d2_pl[i - 1][:], "d2_int")
+                dq_int[i] = d_int(v[:, u[0], u[1]], "dq_int")
+                if i == 1:
+                    g_quant(1)
+                    nc.vector.tensor_tensor(out=sq_in[:, 0 : G * T], in0=p_sb[:], in1=s_abs[:], op=ALU.mult)
+                    nc.gpsimd.tensor_tensor(out=root[:, 0 : G * T], in0=sq_in[:, 0 : G * T], in1=half[:, 0 : G * T], op=ALU.pow)
+                    xp_mul(0)
+                if i == 2:
+                    x2_start(0)
+                    run(x2_ops[0])
+                    x_ints(0)
+                    run(xp_io[0])
+                if i == 3:
+                    xp_q[0] = x_quant(xp_dst[0], CHUNKS[0], "xp")
+                    run(x2_io[0])
+                if i > 0:
+                    d_quant(UNITS[i - 1], d2_int[i - 1], d2_codes, d2_scales)
+                d_quant(u, dq_int[i], dq_codes, dq_scales)
+                if i + 1 < 4:
+                    banks = back(UNITS[i + 1])
+            x2_q[0] = x_quant(x2_dst[0], CHUNKS[0], "x2")
+            d2_int[3] = d_int(d2_pl[3][:], "d2_int")
+            xp_mul(1)
+            d_quant(UNITS[3], d2_int[3], d2_codes, d2_scales)
+            x2_start(1)
+            run(x2_ops[1])
+
+            blocks = {}
+
+            def products(c, pairs):
+                for k in pairs:
+                    m, hb = divmod(k, 2)
+                    blocks[c, k] = [product(x2_q[c], CHUNKS[c], m, d2_codes, d2_scales, hb)]
+                for k in pairs:
+                    m, hb = divmod(k, 2)
+                    blocks[c, k].append(product(xp_q[c], CHUNKS[c], m, dq_codes, dq_scales, hb))
+
+            def products_of(c):
+                n = 2 * CHUNKS[c] // P
+                for k in range(0, n, 2):
+                    products(c, (k, k + 1))
+
+            products_of(0)
+            for c in range(len(CHUNKS)):
+                n = 2 * CHUNKS[c] // P
+                v_ops, s_ops = [], []
+                if c + 1 < len(CHUNKS):
+                    nx = c + 1
+                    x_ints(nx)
+
+                    def q2(nx=nx):
+                        x2_q[nx] = x_quant(x2_dst[nx], CHUNKS[nx], "x2")
+
+                    def qp(nx=nx):
+                        xp_q[nx] = x_quant(xp_dst[nx], CHUNKS[nx], "xp")
+
+                    v_ops += x2_io[nx] + xp_io[nx][:1] + [q2] + xp_io[nx][1:]
+                    late = [qp]
+                    if c + 2 < len(CHUNKS):
+                        x2_start(c + 2)
+                        s_ops = x2_ops[c + 2]
+                else:
+                    late = []
+                done_v = done_s = 0
+                r_of = {}
+                for k in range(n):
+                    fb, gb = blocks[c, k]
+                    r_of[k] = ars(fb)
+                    upto = (k + 1) * len(s_ops) // n
+                    for op in s_ops[done_s:upto]:
+                        op()
+                    done_s = upto
+                    m, hb = divmod(k, 2)
+                    upto = min(len(v_ops), -(-(k + 1) * len(v_ops) // max(n - 1, 1)))
+                    for op in v_ops[done_v:upto]:
+                        op()
+                    done_v = upto
+                    if k == n - 1:
+                        for op in late:
+                            op()
+                    if c == len(CHUNKS) - 1:
+                        finish_twice(gb, r_of[k], starts[c] + m * P, hb)
+                    else:
+                        finish(gb, square_r(r_of[k]), starts[c] + m * P, hb)
+                if c + 1 < len(CHUNKS):
+                    products_of(c + 1)

@@ -22,8 +22,9 @@ P = 128
 T = 4
 G = 2
 HB = 512
-UNITS = [(0, 0), (0, 1), (1, 0), (1, 1)]
-CHUNKS = [256, 256, 256, 128, 128]
+W = 256
+N_CHUNKS = D // W
+PLANES = G * T
 
 
 def tile_diagonalfishernaturalgradient_w4_kernel(tc, x, a, g_bytes, g_scale, w2_words, w2_scales, p, q, s, out):
@@ -34,110 +35,109 @@ def tile_diagonalfishernaturalgradient_w4_kernel(tc, x, a, g_bytes, g_scale, w2_
         epi = ctx.enter_context(tc.tile_pool(name="epi", bufs=4))
         psum = ctx.enter_context(tc.psum_pool(name="psum", bufs=8))
 
-        g_raw = keep.tile([P, G, T, O], U8, align_bytes=64)
-        g_sc = keep.tile([P, O], F32, align_bytes=64)
-        g_bf = keep.tile([P, G, T, O], BF16, align_bytes=64)
-        g_int = keep.tile([P, G * T * O], BF16, align_bytes=64)
-        g_codes = keep.tile([P, G * T * P], U32, align_bytes=64)
-        g_scales = keep.tile([P, G * T * P], U8, align_bytes=64)
+        g_raw = keep.tile([P, PLANES, O], U8, align_bytes=64)
+        g_sc = keep.tile([P, T], F32)
+        g_bf = keep.tile([P, PLANES, O], BF16, align_bytes=64)
+        g_int = keep.tile([P, PLANES, P, T], BF16, align_bytes=64)
+        g_codes = keep.tile([P, PLANES * P], U32, align_bytes=64)
+        g_scales = keep.tile([P, PLANES * P], U8, align_bytes=64)
         w_sb = keep.tile([P, 2 * H], U8, align_bytes=64)
         w_scl = keep.tile([P, H], U8, align_bytes=64)
-        a_sb = keep.tile([P, G, T, H], BF16, align_bytes=64)
-        x_sb = keep.tile([P, G, T, D], BF16, align_bytes=64)
-        xp_pl = keep.tile([P, G, T, D], BF16, align_bytes=64)
-        v = keep.tile([P, G, 2, T, HB], F32, align_bytes=64)
+        a_sb = keep.tile([P, PLANES, H], BF16, align_bytes=64)
+        x_sb = keep.tile([P, PLANES, D], BF16, align_bytes=64)
+        v = keep.tile([P, PLANES, H], F32, align_bytes=64)
+        d2_pl = keep.tile([P, PLANES, H], BF16, align_bytes=64)
+        x2_pl = keep.tile([P, PLANES, D], BF16, align_bytes=64)
         dq_codes = keep.tile([P, G, H], U32, align_bytes=64)
         dq_scales = keep.tile([P, G, H], U8, align_bytes=64)
         d2_codes = keep.tile([P, G, H], U32, align_bytes=64)
         d2_scales = keep.tile([P, G, H], U8, align_bytes=64)
-        p_sb = keep.tile([P, G * T], BF16)
-        q_sb = keep.tile([P, G * T], BF16)
-        s_sb = keep.tile([P, G * T], BF16)
-        s_abs = keep.tile([P, G * T], F32)
-        q_inv = keep.tile([P, G * T], F32)
-        sq_in = keep.tile([P, 3 * G * T], F32)
-        half = keep.tile([P, 3 * G * T], F32)
-        root = keep.tile([P, 3 * G * T], F32)
+        p_sb = keep.tile([P, PLANES], BF16)
+        q_sb = keep.tile([P, PLANES], BF16)
+        s_sb = keep.tile([P, PLANES], BF16)
+        s_abs = keep.tile([P, PLANES], F32)
+        q_inv = keep.tile([P, PLANES], F32)
+        sq_in = keep.tile([P, 3 * PLANES], F32)
+        half = keep.tile([P, 3 * PLANES], F32)
+        root = keep.tile([P, 3 * PLANES], F32)
         ident = keep.tile([P, P], F32)
+        ident_bf = keep.tile([P, P], BF16)
         warm = keep.tile([P, 1], F32)
 
+        def col(tile, j):
+            return tile[:, j : j + 1]
+
         with tc.manual_schedule():
-            x_v = x.rearrange("(g p t) d -> p g t d", g=G, t=T)
-            a_v = a.rearrange("(g p t) h -> p g t h", g=G, t=T)
-            g_v = g_bytes.rearrange("(g p t) o -> p g t o", g=G, t=T)
+            def per_sample(vec):
+                return vec.rearrange("(g p t) -> p g t", g=G, t=T)
+
+            def planes(mat):
+                return mat.rearrange("(g p t) d -> p g t d", g=G, t=T)
+
+            def load_planes(dst, src, j0, n):
+                g, t = divmod(j0, T)
+                nc.sync.dma_start(out=dst[:, j0 : j0 + n], in_=planes(src)[:, g, t : t + n])
+
             nc.gpsimd.memset(w_scl[:].bitcast(U32), 0)
             nc.gpsimd.memset(half[:], 0.5)
             make_identity(nc, ident[:])
             nc.vector.memset(warm[:], 0.0)
-            nc.scalar.dma_start(out=g_sc[:], in_=g_scale.rearrange("o k -> (o k)").partition_broadcast(P))
-            nc.sync.dma_start(out=g_raw[:, 0], in_=g_v[:, 0])
-
-            def load_vector(dst, src):
-                nc.scalar.dma_start(out=dst[:].rearrange("p (g t) -> p g t", g=G), in_=src.rearrange("(g p t) -> p g t", g=G, t=T))
-
-            load_vector(q_sb, q)
-            load_vector(s_sb, s)
+            nc.scalar.dma_start(out=g_sc[:], in_=g_scale.rearrange("o (p t) -> p (o t)", t=T))
+            for dst, src in ((q_sb, q), (s_sb, s)):
+                nc.scalar.dma_start(out=dst[:].rearrange("p (g t) -> p g t", g=G), in_=per_sample(src))
             nc.scalar.activation(out=warm[:], in_=warm[:], func=ACT.Tanh)
-            for t in (0, 2):
-                nc.sync.dma_start(out=a_sb[:, 0, t : t + 2], in_=a_v[:, 0, t : t + 2])
+            load_planes(g_raw, g_bytes, 0, T)
+            load_planes(a_sb, a, 0, 1)
+            load_planes(a_sb, a, 1, 1)
             nc.sync.dma_start(out=w_sb[:], in_=w2_words[0])
+            load_planes(a_sb, a, 2, 2)
             for quad in range(4):
                 nc.sync.dma_start(out=w_scl[32 * quad : 32 * quad + 4, :].bitcast(I32), in_=w2_scales[0, 4 * quad : 4 * quad + 4, :].bitcast(I32))
-            nc.sync.dma_start(out=p_sb[:].rearrange("p (g t) -> p g t", g=G), in_=p.rearrange("(g p t) -> p g t", g=G, t=T))
-            nc.sync.dma_start(out=g_raw[:, 1], in_=g_v[:, 1])
-            for t in (0, 2):
-                nc.sync.dma_start(out=a_sb[:, 1, t : t + 2], in_=a_v[:, 1, t : t + 2])
-            for g in range(G):
-                for t in (0, 2):
-                    nc.sync.dma_start(out=x_sb[:, g, t : t + 2], in_=x_v[:, g, t : t + 2])
+            load_planes(g_raw, g_bytes, T, T)
+            nc.sync.dma_start(out=p_sb[:].rearrange("p (g t) -> p g t", g=G), in_=per_sample(p))
+            load_planes(x_sb, x, 0, T)
+            load_planes(a_sb, a, T, T)
+            load_planes(x_sb, x, T, T)
 
-            def g_mul(g, t):
-                nc.vector.tensor_tensor(out=g_bf[:, g, t], in0=g_raw[:, g, t].bitcast(FP8), in1=g_sc[:], op=ALU.mult)
+            def widen(j0, n):
+                nc.vector.tensor_copy(out=g_bf[:, j0 : j0 + n], in_=g_raw[:, j0 : j0 + n].bitcast(FP8))
 
-            def g_turn(g, t0):
-                bank = psum.tile([P, HB], F32, name="bank")
+            def g_turn(j0):
+                bank = psum.tile([P, 512], F32, name="bank")
                 for i in range(2):
-                    words = g_bf[:, g, t0 + i].bitcast(F32)
+                    words = g_bf[:, j0 + i].bitcast(F32)
                     for u in range(2):
-                        col = (2 * i + u) * P
-                        nc.tensor.transpose(bank[:, col : col + P], words[:, u : O // 2 : 2], ident[:])
+                        c0 = (2 * i + u) * P
+                        nc.tensor.transpose(bank[:, c0 : c0 + P], words[:, u : O // 2 : 2], ident[:])
                 return bank
 
-            def g_out(bank, g, t0):
-                base = (g * T + t0) * O
-                nc.scalar.copy(
-                    out=g_int[:, base : base + 2 * O].bitcast(F32).rearrange("p (i r u) -> p i r u", i=2, u=2),
-                    in_=bank[:].rearrange("p (i u r) -> p i r u", i=2, u=2),
+            def g_mul(bank, i, j):
+                nc.vector.tensor_tensor(
+                    out=g_int[:, j].rearrange("p r (u e) -> p r u e", u=2),
+                    in0=bank[:].bitcast(BF16)[:, i * 512 : (i + 1) * 512].rearrange("p (u r e) -> p r u e", u=2, e=2),
+                    in1=g_sc[:].rearrange("p (u e) -> p u e", u=2).unsqueeze(1).to_broadcast([P, P, 2, 2]),
+                    op=ALU.mult,
                 )
 
-            def g_quant(g):
-                c0 = g * T * P
-                nc.vector.quantize_mx(
-                    out=g_codes[:, c0 : c0 + T * P].bitcast(FP8X4),
-                    scales=g_scales[:, c0 : c0 + T * P],
-                    in_=g_int[:, T * c0 : T * (c0 + T * P)],
-                )
+            def g_quant(j0, n):
+                cs = slice(j0 * P, (j0 + n) * P)
+                nc.vector.quantize_mx(out=g_codes[:, cs].bitcast(FP8X4), scales=g_scales[:, cs], in_=g_int[:, j0 : j0 + n].rearrange("p j r t -> p (j r t)"))
 
-            def tanh(u, t0, n):
-                g, hb = u
-                nc.scalar.activation(out=v[:, g, hb, t0 : t0 + n], in_=a_sb[:, g, t0 : t0 + n, hb * HB : (hb + 1) * HB], func=ACT.Tanh)
+            def tanh(j):
+                nc.scalar.activation(out=v[:, j], in_=a_sb[:, j], func=ACT.Tanh)
 
-            def tanh_sq(u):
-                g, hb = u
-                for t in range(T):
-                    j = 2 * G * T + g * T + t
-                    nc.scalar.activation(out=v[:, g, hb, t], in_=v[:, g, hb, t], func=ACT.Square, scale=root[:, j : j + 1])
+            def tanh_sq(j):
+                nc.scalar.activation(out=v[:, j], in_=v[:, j], func=ACT.Square, scale=col(root, 2 * PLANES + j))
 
-            def back(u):
-                g, hb = u
+            def back(j):
                 banks = []
-                for t in range(T):
-                    bank = psum.tile([P, HB], F32, name="bank")
-                    c0 = (g * T + t) * P
+                cs = slice(j * P, (j + 1) * P)
+                for hb in range(2):
+                    bank = psum.tile([P, 512], F32, name="bank")
                     nc.tensor.matmul_mx(
                         out=bank[:],
-                        lhsT=g_codes[:, c0 : c0 + P].bitcast(FP8X4),
-                        lhsT_scale=g_scales[:, c0 : c0 + P],
+                        lhsT=g_codes[:, cs].bitcast(FP8X4),
+                        lhsT_scale=g_scales[:, cs],
                         rhs=w_sb[:, 2 * hb * HB : 2 * (hb + 1) * HB].bitcast(FP4X4),
                         rhs_scale=w_scl[:, hb * HB : (hb + 1) * HB],
                         start=True,
@@ -146,81 +146,64 @@ def tile_diagonalfishernaturalgradient_w4_kernel(tc, x, a, g_bytes, g_scale, w2_
                     banks.append(bank)
                 return banks
 
-            def v_mul(u, banks):
-                g, hb = u
-                for t in range(T):
-                    j = 2 * G * T + g * T + t
+            def v_mul(j, banks):
+                for hb in range(2):
+                    hs = slice(hb * HB, (hb + 1) * HB)
                     nc.vector.scalar_tensor_tensor(
-                        out=v[:, g, hb, t], in0=v[:, g, hb, t], scalar=sq_in[:, j : j + 1], in1=banks[t][:], op0=ALU.subtract, op1=ALU.mult
+                        out=v[:, j, hs], in0=v[:, j, hs], scalar=col(sq_in, 2 * PLANES + j), in1=banks[hb][:], op0=ALU.subtract, op1=ALU.mult
                     )
 
-            def d2_square(u):
-                g, hb = u
-                d2_pl = work.tile([P, T, HB], BF16, align_bytes=64, name="d2_pl")
-                for t in range(T):
-                    j = G * T + g * T + t
-                    nc.scalar.activation(out=d2_pl[:, t], in_=v[:, g, hb, t], func=ACT.Square, scale=root[:, j : j + 1])
-                return d2_pl
+            def d2_square(j):
+                nc.scalar.activation(out=d2_pl[:, j], in_=v[:, j], func=ACT.Square, scale=col(root, PLANES + j))
+
+            def x2_square(j, half_no):
+                ds = slice(half_no * 512, (half_no + 1) * 512)
+                nc.scalar.activation(out=x2_pl[:, j, ds], in_=x_sb[:, j, ds], func=ACT.Square, scale=col(root, j))
 
             def interleave(dst, src):
                 nc.vector.tensor_copy(out=dst.rearrange("p (c i) t -> p c t i", i=4), in_=src.rearrange("p t (c i) -> p c t i", i=4))
 
-            def d_int(src, name):
-                dst = work.tile([P, HB, T], BF16, align_bytes=64, name=name)
-                interleave(dst[:], src)
+            def d_int(src, g, hb, name):
+                dst = work.tile([P, HB, T], BF16, align_bytes=64, name=name, bufs=2)
+                interleave(dst[:], src[:, T * g : T * (g + 1), hb * HB : (hb + 1) * HB])
                 return dst
 
-            def d_quant(u, src, codes, scales):
-                g, hb = u
-                cols = slice(hb * HB, (hb + 1) * HB)
-                nc.vector.quantize_mx(out=codes[:, g, cols].bitcast(FP8X4), scales=scales[:, g, cols], in_=src[:].rearrange("p n t -> p (n t)"))
+            def d_quant(src, g, hb, codes, scales):
+                hs = slice(hb * HB, (hb + 1) * HB)
+                nc.vector.quantize_mx(out=codes[:, g, hs].bitcast(FP8X4), scales=scales[:, g, hs], in_=src[:].rearrange("p n t -> p (n t)"))
 
-            nc.scalar.activation(out=s_abs[:], in_=s_sb[:], func=ACT.Abs)
-            qs = slice(2 * G * T, 3 * G * T)
-            nc.vector.tensor_scalar(out=sq_in[:, qs], in0=q_sb[:], scalar1=1e-30, scalar2=None, op0=ALU.max)
-            nc.vector.reciprocal(out=q_inv[:], in_=sq_in[:, qs])
-            nc.vector.tensor_tensor(out=sq_in[:, G * T : 2 * G * T], in0=q_inv[:], in1=s_abs[:], op=ALU.mult)
-            dsl = slice(G * T, 3 * G * T)
-            nc.gpsimd.tensor_tensor(out=root[:, dsl], in0=sq_in[:, dsl], in1=half[:, dsl], op=ALU.pow)
+            def x_turn(c, g):
+                bank = psum.tile([P, 512], F32, name="bank")
+                for i in range(2):
+                    d0 = c * W + i * P
+                    nc.tensor.matmul(
+                        bank[:].bitcast(BF16)[:, i * 512 : (i + 1) * 512].rearrange("p (n t) -> p n t", t=T),
+                        lhsT=ident_bf[:],
+                        rhs=x_sb[:, T * g : T * (g + 1), d0 : d0 + P].rearrange("p t n -> p n t"),
+                        start=True,
+                        stop=True,
+                    )
+                return bank
 
-            starts = [sum(CHUNKS[:i]) for i in range(len(CHUNKS))]
-
-            def xp_mul(half_no):
-                cols = slice(half_no * 512, (half_no + 1) * 512)
-                for g in range(G):
-                    for t in range(T):
-                        j = g * T + t
-                        nc.vector.tensor_scalar(out=xp_pl[:, g, t, cols], in0=x_sb[:, g, t, cols], scalar1=p_sb[:, j : j + 1], scalar2=None, op0=ALU.mult)
-
-            def x2_square(c):
-                d0, w = starts[c], CHUNKS[c]
-                x2_pl = work.tile([P, G, T, 256], BF16, align_bytes=64, name="x2_pl", bufs=3)
-
-                def one(g, t):
-                    j = g * T + t
-                    nc.scalar.activation(out=x2_pl[:, g, t, 0:w], in_=x_sb[:, g, t, d0 : d0 + w], func=ACT.Square, scale=root[:, j : j + 1])
-
-                return x2_pl, [lambda g=g, t=t: one(g, t) for g in range(G) for t in range(T)]
-
-            def x_int(src, w, name):
-                dst = work.tile([P, G, 256, T], BF16, align_bytes=64, name=name)
-                return dst, [lambda g=g: interleave(dst[:].rearrange("p g n t -> p (g n) t")[:, g * w : (g + 1) * w, :], src[:, g]) for g in range(G)]
-
-            def x_quant(src, w, name):
-                codes = work.tile([P, G * 256], U32, align_bytes=64, name=name + "_codes")
-                scales = work.tile([P, G * 256], U8, align_bytes=64, name=name + "_scales")
-                nc.vector.quantize_mx(
-                    out=codes[:, 0 : G * w].bitcast(FP8X4),
-                    scales=scales[:, 0 : G * w],
-                    in_=src[:].rearrange("p g n t -> p (g n t)")[:, 0 : G * w * T],
+            def xp_mul(bank, g, dst):
+                nc.vector.tensor_tensor(
+                    out=dst[:, g],
+                    in0=bank[:].bitcast(BF16).rearrange("p (n t) -> p n t", t=T),
+                    in1=p_sb[:, T * g : T * (g + 1)].unsqueeze(1).to_broadcast([P, W, T]),
+                    op=ALU.mult,
                 )
+
+            def x_quant(src, name):
+                codes = work.tile([P, G * W], U32, align_bytes=64, name=name + "_codes", bufs=3)
+                scales = work.tile([P, G * W], U8, align_bytes=64, name=name + "_scales", bufs=3)
+                nc.vector.quantize_mx(out=codes[:].bitcast(FP8X4), scales=scales[:], in_=src[:].rearrange("p g n t -> p (g n t)"))
                 return codes, scales
 
-            def product(lhs, w, m, rhs_codes, rhs_scales, hb):
-                bank = psum.tile([P, HB], F32, name="bank")
+            def product(lhs, m, rhs_codes, rhs_scales, hb):
+                bank = psum.tile([P, 512], F32, name="bank")
                 codes, scales = lhs
                 for g in range(G):
-                    c0 = g * w + m * P
+                    c0 = g * W + m * P
                     nc.tensor.matmul_mx(
                         out=bank[:],
                         lhsT=codes[:, c0 : c0 + P].bitcast(FP8X4),
@@ -242,140 +225,182 @@ def tile_diagonalfishernaturalgradient_w4_kernel(tc, x, a, g_bytes, g_scale, w2_
                 nc.scalar.activation(out=r2[:], in_=r[:], func=ACT.Square)
                 return r2
 
-            def finish(gb, r2, d0, hb):
-                y = epi.tile([P, HB], F32, name="y")
-                nc.vector.scalar_tensor_tensor(out=y[:], in0=gb[:], scalar=-1.0 / 32.0, in1=r2[:], op0=ALU.mult, op1=ALU.mult)
+            def grad_times(gb, r):
+                y = epi.tile([P, HB], F32, name="y", bufs=8)
+                nc.vector.scalar_tensor_tensor(out=y[:], in0=gb[:], scalar=-1.0 / 32.0, in1=r[:], op0=ALU.mult, op1=ALU.mult)
+                return y
+
+            def times(y, r):
+                nc.vector.tensor_tensor(out=y[:], in0=y[:], in1=r[:], op=ALU.mult)
+                return y
+
+            def store(y, d0, hb):
                 nc.sync.dma_start(out=out[d0 : d0 + P, hb * HB : (hb + 1) * HB], in_=y[:])
 
-            def finish_twice(gb, r, d0, hb):
-                y = epi.tile([P, HB], F32, name="y")
-                nc.vector.scalar_tensor_tensor(out=y[:], in0=gb[:], scalar=-1.0 / 32.0, in1=r[:], op0=ALU.mult, op1=ALU.mult)
-                z = epi.tile([P, HB], F32, name="z")
-                nc.vector.tensor_tensor(out=z[:], in0=y[:], in1=r[:], op=ALU.mult)
-                nc.sync.dma_start(out=out[d0 : d0 + P, hb * HB : (hb + 1) * HB], in_=z[:])
+            nc.scalar.activation(out=s_abs[:], in_=s_sb[:], func=ACT.Abs)
+            qs = slice(2 * PLANES, 3 * PLANES)
+            nc.vector.tensor_scalar(out=sq_in[:, qs], in0=q_sb[:], scalar1=1e-30, scalar2=None, op0=ALU.max)
+            nc.vector.reciprocal(out=q_inv[:], in_=sq_in[:, qs])
+            nc.vector.tensor_tensor(out=sq_in[:, PLANES : 2 * PLANES], in0=q_inv[:], in1=s_abs[:], op=ALU.mult)
 
-            x2_planes, x2_ops, x2_dst, xp_dst, x2_io, xp_io, x2_q, xp_q = {}, {}, {}, {}, {}, {}, {}, {}
+            def take_root(c0, c1):
+                nc.gpsimd.tensor_tensor(out=root[:, c0:c1], in0=sq_in[:, c0:c1], in1=half[:, c0:c1], op=ALU.pow)
 
-            def x2_start(c):
-                x2_planes[c], x2_ops[c] = x2_square(c)
+            take_root(PLANES, 3 * PLANES)
+            nc.gpsimd.tensor_copy(out=ident_bf[:], in_=ident[:])
 
-            def x_ints(c):
-                d0, w = starts[c], CHUNKS[c]
-                x2_dst[c], x2_io[c] = x_int(x2_planes[c][:, :, :, 0:w], w, "x2_int")
-                xp_dst[c], xp_io[c] = x_int(xp_pl[:, :, :, d0 : d0 + w], w, "xp_int")
-
-            def run(ops):
-                for op in ops:
-                    op()
-
-            for t in range(T):
-                g_mul(0, t)
-            tanh(UNITS[0], 0, 2)
-            g_out(g_turn(0, 0), 0, 0)
-            tanh(UNITS[0], 2, 2)
-            g_out(g_turn(0, 2), 0, 2)
-            g_quant(0)
-            tanh_sq(UNITS[0])
-            banks = back(UNITS[0])
-            d2_pl, dq_int, d2_int = {}, {}, {}
-            for i in range(4):
-                u = UNITS[i]
-                v_mul(u, banks)
-                if i == 0:
-                    for t in range(T):
-                        g_mul(1, t)
-                    turned = [g_turn(1, 0), g_turn(1, 2)]
-                if i + 1 < 4:
-                    tanh(UNITS[i + 1], 0, T)
-                    tanh_sq(UNITS[i + 1])
-                if i == 0:
-                    g_out(turned[0], 1, 0)
-                    g_out(turned[1], 1, 2)
-                d2_pl[i] = d2_square(u)
-                if i > 0:
-                    d2_int[i - 1] = d_int(d2_pl[i - 1][:], "d2_int")
-                dq_int[i] = d_int(v[:, u[0], u[1]], "dq_int")
-                if i == 1:
-                    g_quant(1)
-                    nc.vector.tensor_tensor(out=sq_in[:, 0 : G * T], in0=p_sb[:], in1=s_abs[:], op=ALU.mult)
-                    nc.gpsimd.tensor_tensor(out=root[:, 0 : G * T], in0=sq_in[:, 0 : G * T], in1=half[:, 0 : G * T], op=ALU.pow)
-                    xp_mul(0)
-                if i == 2:
-                    x2_start(0)
-                    run(x2_ops[0])
-                    x_ints(0)
-                    run(xp_io[0])
-                if i == 3:
-                    xp_q[0] = x_quant(xp_dst[0], CHUNKS[0], "xp")
-                    run(x2_io[0])
-                if i > 0:
-                    d_quant(UNITS[i - 1], d2_int[i - 1], d2_codes, d2_scales)
-                d_quant(u, dq_int[i], dq_codes, dq_scales)
-                if i + 1 < 4:
-                    banks = back(UNITS[i + 1])
-            x2_q[0] = x_quant(x2_dst[0], CHUNKS[0], "x2")
-            d2_int[3] = d_int(d2_pl[3][:], "d2_int")
-            xp_mul(1)
-            d_quant(UNITS[3], d2_int[3], d2_codes, d2_scales)
-            x2_start(1)
-            run(x2_ops[1])
-
-            blocks = {}
-
-            def products(c, pairs):
-                for k in pairs:
-                    m, hb = divmod(k, 2)
-                    blocks[c, k] = [product(x2_q[c], CHUNKS[c], m, d2_codes, d2_scales, hb)]
-                for k in pairs:
-                    m, hb = divmod(k, 2)
-                    blocks[c, k].append(product(xp_q[c], CHUNKS[c], m, dq_codes, dq_scales, hb))
-
-            def products_of(c):
-                n = 2 * CHUNKS[c] // P
-                for k in range(0, n, 2):
-                    products(c, (k, k + 1))
-
-            products_of(0)
-            for c in range(len(CHUNKS)):
-                n = 2 * CHUNKS[c] // P
-                v_ops, s_ops = [], []
-                if c + 1 < len(CHUNKS):
-                    nx = c + 1
-                    x_ints(nx)
-
-                    def q2(nx=nx):
-                        x2_q[nx] = x_quant(x2_dst[nx], CHUNKS[nx], "x2")
-
-                    def qp(nx=nx):
-                        xp_q[nx] = x_quant(xp_dst[nx], CHUNKS[nx], "xp")
-
-                    v_ops += x2_io[nx] + xp_io[nx][:1] + [q2] + xp_io[nx][1:]
-                    late = [qp]
-                    if c + 2 < len(CHUNKS):
-                        x2_start(c + 2)
-                        s_ops = x2_ops[c + 2]
+            def d_step(kind, g, hb):
+                src, codes, scales = (v, dq_codes, dq_scales) if kind == "dq" else (d2_pl, d2_codes, d2_scales)
+                if (kind, g, hb) not in ints:
+                    ints[kind, g, hb] = d_int(src, g, hb, kind + "_int")
                 else:
-                    late = []
-                done_v = done_s = 0
-                r_of = {}
-                for k in range(n):
-                    fb, gb = blocks[c, k]
-                    r_of[k] = ars(fb)
-                    upto = (k + 1) * len(s_ops) // n
-                    for op in s_ops[done_s:upto]:
-                        op()
-                    done_s = upto
-                    m, hb = divmod(k, 2)
-                    upto = min(len(v_ops), -(-(k + 1) * len(v_ops) // max(n - 1, 1)))
-                    for op in v_ops[done_v:upto]:
-                        op()
-                    done_v = upto
-                    if k == n - 1:
-                        for op in late:
-                            op()
-                    if c == len(CHUNKS) - 1:
-                        finish_twice(gb, r_of[k], starts[c] + m * P, hb)
-                    else:
-                        finish(gb, square_r(r_of[k]), starts[c] + m * P, hb)
-                if c + 1 < len(CHUNKS):
-                    products_of(c + 1)
+                    d_quant(ints[kind, g, hb], g, hb, codes, scales)
+
+            ints = {}
+            xp_int = {}
+
+            def xp(c, g):
+                if c not in xp_int:
+                    dst = work.tile([P, G, W, T], BF16, align_bytes=64, name="xp_int", bufs=N_CHUNKS)
+                    xp_int[c] = dst
+                xp_mul(x_turn(c, g), g, xp_int[c])
+
+            widen(0, 2)
+            b0 = g_turn(0)
+            widen(2, 2)
+            b1 = g_turn(2)
+            tanh(0)
+            tanh(1)
+            g_mul(b0, 0, 0)
+            g_mul(b0, 1, 1)
+            tanh_sq(0)
+            g_mul(b1, 0, 2)
+            g_quant(0, 2)
+            g_mul(b1, 1, 3)
+            banks = back(0)
+            g_quant(2, 2)
+            for j in range(PLANES):
+                if j + 2 < PLANES:
+                    tanh(j + 2)
+                if j > 0:
+                    d2_square(j - 1)
+                if j + 1 < PLANES:
+                    tanh_sq(j + 1)
+                v_mul(j, banks)
+                if j + 1 < PLANES:
+                    banks = back(j + 1)
+                if j == 0:
+                    widen(4, 2)
+                    b0 = g_turn(4)
+                    widen(6, 2)
+                    b1 = g_turn(6)
+                if j == 1:
+                    g_mul(b0, 0, 4)
+                    g_mul(b0, 1, 5)
+                if j == 2:
+                    g_mul(b1, 0, 6)
+                    g_quant(4, 2)
+                    g_mul(b1, 1, 7)
+                    xp(0, 0)
+                    g_quant(6, 2)
+                if j == 3:
+                    nc.vector.tensor_tensor(out=sq_in[:, 0:PLANES], in0=p_sb[:], in1=s_abs[:], op=ALU.mult)
+                    take_root(0, PLANES)
+                    xp(1, 0)
+                    xp(2, 0)
+                if j == 4:
+                    d_step("dq", 0, 0)
+                    d_step("dq", 0, 1)
+                if j == 5:
+                    d_step("d2", 0, 0)
+                    d_step("dq", 0, 0)
+                    d_step("dq", 0, 1)
+                if j == 6:
+                    d_step("d2", 0, 1)
+                    d_step("d2", 0, 0)
+                    xp(0, 1)
+                if j == 7:
+                    d_step("d2", 0, 1)
+                    xp(3, 0)
+            x2_square(0, 0)
+            d2_square(PLANES - 1)
+            d_step("dq", 1, 0)
+            d_step("d2", 1, 0)
+            d_step("dq", 1, 0)
+            d_step("d2", 1, 1)
+            d_step("d2", 1, 0)
+            for j in range(1, PLANES):
+                x2_square(j, 0)
+
+            x2_int, x2_q, xp_q = {}, {}, {}
+
+            def x2(c, g):
+                if c not in x2_int:
+                    dst = work.tile([P, G, W, T], BF16, align_bytes=64, name="x2_int")
+                    x2_int[c] = dst
+                interleave(x2_int[c][:, g], x2_pl[:, T * g : T * (g + 1), c * W : (c + 1) * W])
+
+            def quant_x2(c):
+                x2_q[c] = x_quant(x2_int[c], "x2")
+
+            def quant_xp(c):
+                xp_q[c] = x_quant(xp_int[c], "xp")
+
+            xp(1, 1)
+            d_step("d2", 1, 1)
+            x2(0, 0)
+            xp(2, 1)
+            xp(3, 1)
+            d_step("dq", 1, 1)
+            x2(0, 1)
+            quant_xp(0)
+            quant_x2(0)
+            d_step("dq", 1, 1)
+
+            BLOCKS = [(m, hb) for m in range(W // P) for hb in range(2)]
+            fisher, grad, roots = {}, {}, {}
+
+            def products(c, k):
+                for m, hb in BLOCKS[k : k + 2]:
+                    fisher[c, m, hb] = product(x2_q[c], m, d2_codes, d2_scales, hb)
+                for m, hb in BLOCKS[k : k + 2]:
+                    grad[c, m, hb] = product(xp_q[c], m, dq_codes, dq_scales, hb)
+
+            products(0, 0)
+            products(0, 2)
+            for j in range(6):
+                x2_square(j, 1)
+            nc.scalar.activation(out=warm[:], in_=warm[:], func=ACT.Abs_reciprocal_sqrt, bias=1.0)
+            s_ops = [(j, 1) for j in range(6, PLANES)]
+            x2(1, 0)
+            x2(1, 1)
+            quant_xp(1)
+            quant_x2(1)
+            order = [(c, m, hb) for c in range(N_CHUNKS) for m, hb in BLOCKS]
+            roots[order[0]] = ars(fisher[order[0]])
+            for b, key in enumerate(order):
+                c, m, hb = key
+                k = b % len(BLOCKS)
+                nx = c + 1
+                if c + 2 < N_CHUNKS:
+                    if k == 1:
+                        x2(c + 2, 0)
+                    if k == 2:
+                        x2(c + 2, 1)
+                        quant_xp(c + 2)
+                    if k == 3:
+                        quant_x2(c + 2)
+                if k == 2 and nx < N_CHUNKS:
+                    products(nx, 0)
+                if b + 1 < len(order):
+                    roots[order[b + 1]] = ars(fisher[order[b + 1]])
+                for j, half_no in s_ops[b : b + 1]:
+                    x2_square(j, half_no)
+                r = roots[key]
+                if c >= 2 and k % 2 == 1:
+                    y = times(grad_times(grad[key], r), r)
+                else:
+                    y = grad_times(grad[key], square_r(r))
+                store(y, c * W + m * P, hb)
+                if k == 3 and nx < N_CHUNKS:
+                    products(nx, 2)

@@ -163,6 +163,19 @@ def tile_diagonalfishernaturalgradient_w4_kernel(tc, x, a, g_bytes, g_scale, w2_
             def interleave(dst, src):
                 nc.vector.tensor_copy(out=dst.rearrange("p (c i) t -> p c t i", i=4), in_=src.rearrange("p t (c i) -> p c t i", i=4))
 
+            def d_int_pool(g, hb):
+                dst = work.tile([P, HB, T], BF16, align_bytes=64, name="d2_int", bufs=2)
+                for n0 in (0, 256):
+                    nc.gpsimd.tensor_scalar(
+                        out=dst[:, n0 : n0 + 256],
+                        in0=d2_pl[:, T * g : T * (g + 1), hb * HB + n0 : hb * HB + n0 + 256].rearrange("p t n -> p n t"),
+                        scalar1=1.0,
+                        scalar2=0.0,
+                        op0=ALU.mult,
+                        op1=ALU.add,
+                    )
+                ints["d2", g, hb] = dst
+
             def d_int(src, g, hb, name):
                 dst = work.tile([P, HB, T], BF16, align_bytes=64, name=name, bufs=2)
                 interleave(dst[:], src[:, T * g : T * (g + 1), hb * HB : (hb + 1) * HB])
@@ -297,31 +310,34 @@ def tile_diagonalfishernaturalgradient_w4_kernel(tc, x, a, g_bytes, g_scale, w2_
                 if j == 1:
                     g_mul(b0, 0, 4)
                     g_mul(b0, 1, 5)
-                if j == 2:
                     g_mul(b1, 0, 6)
+                if j == 2:
                     g_quant(4, 2)
                     g_mul(b1, 1, 7)
                     xp(0, 0)
+                    xp(1, 0)
                     g_quant(6, 2)
                 if j == 3:
                     nc.vector.tensor_tensor(out=sq_in[:, 0:PLANES], in0=p_sb[:], in1=s_abs[:], op=ALU.mult)
                     take_root(0, PLANES)
-                    xp(1, 0)
                     xp(2, 0)
+                    xp(3, 0)
+                    d_step("dq", 0, 0)
                 if j == 4:
-                    d_step("dq", 0, 0)
+                    d_int_pool(0, 0)
+                    d_int_pool(0, 1)
                     d_step("dq", 0, 1)
-                if j == 5:
-                    d_step("d2", 0, 0)
                     d_step("dq", 0, 0)
+                if j == 5:
+                    xp(0, 1)
+                    xp(1, 1)
                     d_step("dq", 0, 1)
                 if j == 6:
-                    d_step("d2", 0, 1)
+                    xp(2, 1)
+                    xp(3, 1)
                     d_step("d2", 0, 0)
-                    xp(0, 1)
                 if j == 7:
                     d_step("d2", 0, 1)
-                    xp(3, 0)
             x2_square(0, 0)
             d2_square(PLANES - 1)
             d_step("dq", 1, 0)
@@ -346,11 +362,8 @@ def tile_diagonalfishernaturalgradient_w4_kernel(tc, x, a, g_bytes, g_scale, w2_
             def quant_xp(c):
                 xp_q[c] = x_quant(xp_int[c], "xp")
 
-            xp(1, 1)
             d_step("d2", 1, 1)
             x2(0, 0)
-            xp(2, 1)
-            xp(3, 1)
             d_step("dq", 1, 1)
             x2(0, 1)
             quant_xp(0)

@@ -82,12 +82,13 @@ def tile_diagonalfishernaturalgradient_w4_kernel(tc, x, a, g_bytes, g_scale, w2_
             nc.gpsimd.memset(half[:], 0.5)
             make_identity(nc, ident[:])
             nc.vector.memset(warm[:], 0.0)
+            nc.scalar.dma_start(out=a_sb[:, 0], in_=planes(a)[:, 0, 0])
             nc.scalar.dma_start(out=g_sc[:], in_=g_scale.rearrange("o (p t) -> p (o t)", t=T))
             for dst, src in ((q_sb, q), (s_sb, s)):
                 nc.scalar.dma_start(out=dst[:].rearrange("p (g t) -> p g t", g=G), in_=per_sample(src))
             nc.scalar.activation(out=warm[:], in_=warm[:], func=ACT.Tanh)
-            load_planes(g_raw, g_bytes, 0, T)
-            load_planes(a_sb, a, 0, 1)
+            load_planes(g_raw, g_bytes, 0, 2)
+            load_planes(g_raw, g_bytes, 2, 2)
             load_planes(a_sb, a, 1, 1)
             nc.sync.dma_start(out=w_sb[:], in_=w2_words[0])
             load_planes(a_sb, a, 2, 2)
@@ -212,21 +213,18 @@ def tile_diagonalfishernaturalgradient_w4_kernel(tc, x, a, g_bytes, g_scale, w2_
                 nc.vector.quantize_mx(out=codes[:].bitcast(FP8X4), scales=scales[:], in_=src[:].rearrange("p g n t -> p (g n t)"))
                 return codes, scales
 
-            def product(lhs, m, rhs_codes, rhs_scales, hb):
-                bank = psum.tile([P, 512], F32, name="bank")
+            def product_pass(bank, lhs, m, rhs_codes, rhs_scales, hb, g):
                 codes, scales = lhs
-                for g in range(G):
-                    c0 = g * W + m * P
-                    nc.tensor.matmul_mx(
-                        out=bank[:],
-                        lhsT=codes[:, c0 : c0 + P].bitcast(FP8X4),
-                        lhsT_scale=scales[:, c0 : c0 + P],
-                        rhs=rhs_codes[:, g, hb * HB : (hb + 1) * HB].bitcast(FP8X4),
-                        rhs_scale=rhs_scales[:, g, hb * HB : (hb + 1) * HB],
-                        start=(g == 0),
-                        stop=(g == G - 1),
-                    )
-                return bank
+                c0 = g * W + m * P
+                nc.tensor.matmul_mx(
+                    out=bank[:],
+                    lhsT=codes[:, c0 : c0 + P].bitcast(FP8X4),
+                    lhsT_scale=scales[:, c0 : c0 + P],
+                    rhs=rhs_codes[:, g, hb * HB : (hb + 1) * HB].bitcast(FP8X4),
+                    rhs_scale=rhs_scales[:, g, hb * HB : (hb + 1) * HB],
+                    start=(g == 0),
+                    stop=(g == G - 1),
+                )
 
             def ars(fb):
                 r = epi.tile([P, HB], F32, name="r")
@@ -241,10 +239,6 @@ def tile_diagonalfishernaturalgradient_w4_kernel(tc, x, a, g_bytes, g_scale, w2_
             def grad_times(gb, r):
                 y = epi.tile([P, HB], F32, name="y", bufs=8)
                 nc.vector.scalar_tensor_tensor(out=y[:], in0=gb[:], scalar=-1.0 / 32.0, in1=r[:], op0=ALU.mult, op1=ALU.mult)
-                return y
-
-            def times(y, r):
-                nc.vector.tensor_tensor(out=y[:], in0=y[:], in1=r[:], op=ALU.mult)
                 return y
 
             def store(y, d0, hb):
@@ -315,35 +309,33 @@ def tile_diagonalfishernaturalgradient_w4_kernel(tc, x, a, g_bytes, g_scale, w2_
                     g_quant(4, 2)
                     g_mul(b1, 1, 7)
                     xp(0, 0)
-                    xp(1, 0)
                     g_quant(6, 2)
+                    xp(1, 0)
                 if j == 3:
                     nc.vector.tensor_tensor(out=sq_in[:, 0:PLANES], in0=p_sb[:], in1=s_abs[:], op=ALU.mult)
                     take_root(0, PLANES)
-                    xp(2, 0)
-                    xp(3, 0)
                     d_step("dq", 0, 0)
+                    d_step("dq", 0, 1)
                 if j == 4:
                     d_int_pool(0, 0)
                     d_int_pool(0, 1)
-                    d_step("dq", 0, 1)
-                    d_step("dq", 0, 0)
-                if j == 5:
                     xp(0, 1)
                     xp(1, 1)
-                    d_step("dq", 0, 1)
-                if j == 6:
+                    xp(2, 0)
+                if j == 5:
                     xp(2, 1)
-                    xp(3, 1)
-                    d_step("d2", 0, 0)
+                    xp(3, 0)
+                if j == 6:
+                    d_step("dq", 0, 0)
+                    d_step("dq", 0, 1)
                 if j == 7:
+                    d_step("d2", 0, 0)
+                    xp(3, 1)
                     d_step("d2", 0, 1)
             x2_square(0, 0)
             d2_square(PLANES - 1)
             d_step("dq", 1, 0)
-            d_step("d2", 1, 0)
-            d_step("dq", 1, 0)
-            d_step("d2", 1, 1)
+            d_step("dq", 1, 1)
             d_step("d2", 1, 0)
             for j in range(1, PLANES):
                 x2_square(j, 0)
@@ -362,29 +354,36 @@ def tile_diagonalfishernaturalgradient_w4_kernel(tc, x, a, g_bytes, g_scale, w2_
             def quant_xp(c):
                 xp_q[c] = x_quant(xp_int[c], "xp")
 
-            d_step("d2", 1, 1)
             x2(0, 0)
-            d_step("dq", 1, 1)
+            d_step("d2", 1, 1)
             x2(0, 1)
-            quant_xp(0)
             quant_x2(0)
-            d_step("dq", 1, 1)
+            quant_xp(0)
 
             BLOCKS = [(m, hb) for m in range(W // P) for hb in range(2)]
             fisher, grad, roots = {}, {}, {}
 
-            def products(c, k):
-                for m, hb in BLOCKS[k : k + 2]:
-                    fisher[c, m, hb] = product(x2_q[c], m, d2_codes, d2_scales, hb)
-                for m, hb in BLOCKS[k : k + 2]:
-                    grad[c, m, hb] = product(xp_q[c], m, dq_codes, dq_scales, hb)
+            def products(c, k, passes=((0, 1),)):
+                for group in passes:
+                    for made, lhs, codes, scales in ((fisher, x2_q, d2_codes, d2_scales), (grad, xp_q, dq_codes, dq_scales)):
+                        for m, hb in BLOCKS[k : k + 2]:
+                            if group[0] == 0:
+                                bank = psum.tile([P, 512], F32, name="bank")
+                                made[c, m, hb] = bank
+                            for g in group:
+                                product_pass(made[c, m, hb], lhs[c], m, codes, scales, hb, g)
 
-            products(0, 0)
-            products(0, 2)
-            for j in range(6):
+            for k in (0, 2):
+                products(0, k, ((0,),))
+            d_step("d2", 1, 0)
+            d_step("d2", 1, 1)
+            d_step("dq", 1, 0)
+            d_step("dq", 1, 1)
+            for k in (0, 2):
+                products(0, k, ((1,),))
+            for j in range(PLANES):
                 x2_square(j, 1)
             nc.scalar.activation(out=warm[:], in_=warm[:], func=ACT.Abs_reciprocal_sqrt, bias=1.0)
-            s_ops = [(j, 1) for j in range(6, PLANES)]
             x2(1, 0)
             x2(1, 1)
             quant_xp(1)
@@ -407,13 +406,8 @@ def tile_diagonalfishernaturalgradient_w4_kernel(tc, x, a, g_bytes, g_scale, w2_
                     products(nx, 0)
                 if b + 1 < len(order):
                     roots[order[b + 1]] = ars(fisher[order[b + 1]])
-                for j, half_no in s_ops[b : b + 1]:
-                    x2_square(j, half_no)
                 r = roots[key]
-                if c >= 2 and k % 2 == 1:
-                    y = times(grad_times(grad[key], r), r)
-                else:
-                    y = grad_times(grad[key], square_r(r))
+                y = grad_times(grad[key], square_r(r))
                 store(y, c * W + m * P, hb)
                 if k == 3 and nx < N_CHUNKS:
                     products(nx, 2)

@@ -157,9 +157,13 @@ def tile_diagonalfishernaturalgradient_w4_kernel(tc, x, a, g_bytes, g_scale, w2_
             def d2_square(j):
                 nc.scalar.activation(out=d2_pl[:, j], in_=v[:, j], func=ACT.Square, scale=col(root, PLANES + j))
 
-            def x2_square(j, half_no):
-                ds = slice(half_no * 512, (half_no + 1) * 512)
-                nc.scalar.activation(out=x2_pl[:, j, ds], in_=x_sb[:, j, ds], func=ACT.Square, scale=col(root, j))
+            def x2_square(j, d0, d1):
+                nc.scalar.activation(out=x2_pl[:, j, d0:d1], in_=x_sb[:, j, d0:d1], func=ACT.Square, scale=col(root, j))
+
+            def x2_vector(j, d0, d1):
+                nc.vector.scalar_tensor_tensor(
+                    out=x2_pl[:, j, d0:d1], in0=x_sb[:, j, d0:d1], scalar=col(sq_in, j), in1=x_sb[:, j, d0:d1], op0=ALU.mult, op1=ALU.mult
+                )
 
             def interleave(dst, src):
                 nc.vector.tensor_copy(out=dst.rearrange("p (c i) t -> p c t i", i=4), in_=src.rearrange("p t (c i) -> p c t i", i=4))
@@ -236,6 +240,11 @@ def tile_diagonalfishernaturalgradient_w4_kernel(tc, x, a, g_bytes, g_scale, w2_
                 nc.scalar.activation(out=r2[:], in_=r[:], func=ACT.Square)
                 return r2
 
+            def square_r_pool(r):
+                r2 = epi.tile([P, HB], F32, name="r2")
+                nc.gpsimd.tensor_tensor(out=r2[:], in0=r[:], in1=r[:], op=ALU.mult)
+                return r2
+
             def grad_times(gb, r):
                 y = epi.tile([P, HB], F32, name="y", bufs=8)
                 nc.vector.scalar_tensor_tensor(out=y[:], in0=gb[:], scalar=-1.0 / 32.0, in1=r[:], op0=ALU.mult, op1=ALU.mult)
@@ -255,6 +264,12 @@ def tile_diagonalfishernaturalgradient_w4_kernel(tc, x, a, g_bytes, g_scale, w2_
 
             take_root(PLANES, 3 * PLANES)
             nc.gpsimd.tensor_copy(out=ident_bf[:], in_=ident[:])
+
+            def scalar_interleave(dst, g, hb, n0):
+                nc.scalar.copy(
+                    out=dst[:, n0 : n0 + 256].rearrange("p (c i) t -> p c t i", i=4),
+                    in_=d2_pl[:, T * g : T * (g + 1), hb * HB + n0 : hb * HB + n0 + 256].rearrange("p t (c i) -> p c t i", i=4),
+                )
 
             def d_step(kind, g, hb):
                 src, codes, scales = (v, dq_codes, dq_scales) if kind == "dq" else (d2_pl, d2_codes, d2_scales)
@@ -332,13 +347,16 @@ def tile_diagonalfishernaturalgradient_w4_kernel(tc, x, a, g_bytes, g_scale, w2_
                     d_step("d2", 0, 0)
                     xp(3, 1)
                     d_step("d2", 0, 1)
-            x2_square(0, 0)
+            x2_square(0, 0, 2 * W)
             d2_square(PLANES - 1)
             d_step("dq", 1, 0)
             d_step("dq", 1, 1)
             d_step("d2", 1, 0)
             for j in range(1, PLANES):
-                x2_square(j, 0)
+                x2_square(j, 0, 2 * W)
+            dst = work.tile([P, HB, T], BF16, align_bytes=64, name="d2_int", bufs=2)
+            ints["d2", 1, 1] = dst
+            scalar_interleave(dst, 1, 1, 256)
 
             x2_int, x2_q, xp_q = {}, {}, {}
 
@@ -355,7 +373,7 @@ def tile_diagonalfishernaturalgradient_w4_kernel(tc, x, a, g_bytes, g_scale, w2_
                 xp_q[c] = x_quant(xp_int[c], "xp")
 
             x2(0, 0)
-            d_step("d2", 1, 1)
+            interleave(ints["d2", 1, 1][:, 0:256], d2_pl[:, T:PLANES, HB : HB + 256])
             x2(0, 1)
             quant_x2(0)
             quant_xp(0)
@@ -381,8 +399,8 @@ def tile_diagonalfishernaturalgradient_w4_kernel(tc, x, a, g_bytes, g_scale, w2_
             d_step("dq", 1, 1)
             for k in (0, 2):
                 products(0, k, ((1,),))
-            for j in range(PLANES):
-                x2_square(j, 1)
+            for j in range(PLANES - 2):
+                x2_square(j, 2 * W, D)
             nc.scalar.activation(out=warm[:], in_=warm[:], func=ACT.Abs_reciprocal_sqrt, bias=1.0)
             x2(1, 0)
             x2(1, 1)
@@ -394,6 +412,8 @@ def tile_diagonalfishernaturalgradient_w4_kernel(tc, x, a, g_bytes, g_scale, w2_
                 c, m, hb = key
                 k = b % len(BLOCKS)
                 nx = c + 1
+                if c == 0 and k < 2:
+                    x2_square(PLANES - 2 + k, 2 * W, D)
                 if c + 2 < N_CHUNKS:
                     if k == 1:
                         x2(c + 2, 0)
@@ -407,7 +427,7 @@ def tile_diagonalfishernaturalgradient_w4_kernel(tc, x, a, g_bytes, g_scale, w2_
                 if b + 1 < len(order):
                     roots[order[b + 1]] = ars(fisher[order[b + 1]])
                 r = roots[key]
-                y = grad_times(grad[key], square_r(r))
+                y = grad_times(grad[key], (square_r_pool if b in (1, 9, 11, 13) else square_r)(r))
                 store(y, c * W + m * P, hb)
                 if k == 3 and nx < N_CHUNKS:
                     products(nx, 2)

from contextlib import ExitStack

import concourse.mybir as mybir
from concourse.masks import make_identity

N, D, H, O = 1024, 1024, 1024, 512
DAMP = 0.2
FLOPS = 2 * N * D * H * 2 + 2 * N * O * H

F32 = mybir.dt.float32
BF16 = mybir.dt.bfloat16
U32 = mybir.dt.uint32
I32 = mybir.dt.int32
U8 = mybir.dt.uint8
FP8 = mybir.dt.float8_e4m3fn
FP8X4 = mybir.dt.float8_e4m3fn_x4
FP4X4 = mybir.dt.float4_e2m1fn_x4
ACT = mybir.ActivationFunctionType
ALU = mybir.AluOpType

P = 128
T = 4
G = 2
HB = 512
W = 256
N_CHUNKS = D // W
PLANES = G * T


def tile_diagonalfishernaturalgradient_w4_kernel(tc, x, a, g_bytes, g_scale, w2_words, w2_scales, p, q, s, out):
    nc = tc.nc
    with ExitStack() as ctx:
        keep = ctx.enter_context(tc.tile_pool(name="keep", bufs=1))
        work = ctx.enter_context(tc.tile_pool(name="work", bufs=2))
        epi = ctx.enter_context(tc.tile_pool(name="epi", bufs=4))
        psum = ctx.enter_context(tc.psum_pool(name="psum", bufs=8))

        g_raw = keep.tile([P, PLANES, O], U8, align_bytes=64)
        g_sc = keep.tile([P, T], F32)
        g_bf = keep.tile([P, PLANES, O], BF16, align_bytes=64)
        g_int = keep.tile([P, PLANES, P, T], BF16, align_bytes=64)
        g_codes = keep.tile([P, PLANES * P], U32, align_bytes=64)
        g_scales = keep.tile([P, PLANES * P], U8, align_bytes=64)
        w_sb = keep.tile([P, 2 * H], U8, align_bytes=64)
        w_scl = keep.tile([P, H], U8, align_bytes=64)
        a_sb = keep.tile([P, PLANES, H], BF16, align_bytes=64)
        x_sb = keep.tile([P, PLANES, D], BF16, align_bytes=64)
        v = keep.tile([P, PLANES, H], F32, align_bytes=64)
        d2_pl = keep.tile([P, PLANES, H], BF16, align_bytes=64)
        x2_pl = keep.tile([P, PLANES, D], BF16, align_bytes=64)
        dq_codes = keep.tile([P, G, H], U32, align_bytes=64)
        dq_scales = keep.tile([P, G, H], U8, align_bytes=64)
        d2_codes = keep.tile([P, G, H], U32, align_bytes=64)
        d2_scales = keep.tile([P, G, H], U8, align_bytes=64)
        p_sb = keep.tile([P, PLANES], BF16)
        q_sb = keep.tile([P, PLANES], BF16)
        s_sb = keep.tile([P, PLANES], BF16)
        s_abs = keep.tile([P, PLANES], F32)
        q_inv = keep.tile([P, PLANES], F32)
        sq_in = keep.tile([P, 3 * PLANES], F32)
        half = keep.tile([P, 3 * PLANES], F32)
        root = keep.tile([P, 3 * PLANES], F32)
        ident = keep.tile([P, P], F32)
        ident_bf = keep.tile([P, P], BF16)
        warm = keep.tile([P, 1], F32)

        def col(tile, j):
            return tile[:, j : j + 1]

        with tc.manual_schedule():
            def per_sample(vec):
                return vec.rearrange("(g p t) -> p g t", g=G, t=T)

            def planes(mat):
                return mat.rearrange("(g p t) d -> p g t d", g=G, t=T)

            def load_planes(dst, src, j0, n):
                g, t = divmod(j0, T)
                nc.sync.dma_start(out=dst[:, j0 : j0 + n], in_=planes(src)[:, g, t : t + n])

            nc.gpsimd.memset(w_scl[:].bitcast(U32), 0)
            nc.gpsimd.memset(half[:], 0.5)
            make_identity(nc, ident[:])
            nc.vector.memset(warm[:], 0.0)
            nc.scalar.dma_start(out=a_sb[:, 0], in_=planes(a)[:, 0, 0])
            nc.scalar.dma_start(out=g_sc[:], in_=g_scale.rearrange("o (p t) -> p (o t)", t=T))
            for dst, src in ((q_sb, q), (s_sb, s)):
                nc.scalar.dma_start(out=dst[:].rearrange("p (g t) -> p g t", g=G), in_=per_sample(src))
            nc.scalar.activation(out=warm[:], in_=warm[:], func=ACT.Tanh)
            load_planes(g_raw, g_bytes, 0, 2)
            load_planes(g_raw, g_bytes, 2, 2)
            load_planes(a_sb, a, 1, 1)
            nc.sync.dma_start(out=w_sb[:], in_=w2_words[0])
            load_planes(a_sb, a, 2, 2)
            for quad in range(4):
                nc.sync.dma_start(out=w_scl[32 * quad : 32 * quad + 4, :].bitcast(I32), in_=w2_scales[0, 4 * quad : 4 * quad + 4, :].bitcast(I32))
            load_planes(g_raw, g_bytes, T, T)
            nc.sync.dma_start(out=p_sb[:].rearrange("p (g t) -> p g t", g=G), in_=per_sample(p))
            load_planes(x_sb, x, 0, T)
            load_planes(a_sb, a, T, T)
            load_planes(x_sb, x, T, T)

            def widen(j0, n):
                nc.vector.tensor_copy(out=g_bf[:, j0 : j0 + n], in_=g_raw[:, j0 : j0 + n].bitcast(FP8))

            def g_turn(j0):
                bank = psum.tile([P, 512], F32, name="bank")
                for i in range(2):
                    words = g_bf[:, j0 + i].bitcast(F32)
                    for u in range(2):
                        c0 = (2 * i + u) * P
                        nc.tensor.transpose(bank[:, c0 : c0 + P], words[:, u : O // 2 : 2], ident[:])
                return bank

            def g_mul(bank, i, j):
                nc.vector.tensor_tensor(
                    out=g_int[:, j].rearrange("p r (u e) -> p r u e", u=2),
                    in0=bank[:].bitcast(BF16)[:, i * 512 : (i + 1) * 512].rearrange("p (u r e) -> p r u e", u=2, e=2),
                    in1=g_sc[:].rearrange("p (u e) -> p u e", u=2).unsqueeze(1).to_broadcast([P, P, 2, 2]),
                    op=ALU.mult,
                )

            def g_quant(j0, n):
                cs = slice(j0 * P, (j0 + n) * P)
                nc.vector.quantize_mx(out=g_codes[:, cs].bitcast(FP8X4), scales=g_scales[:, cs], in_=g_int[:, j0 : j0 + n].rearrange("p j r t -> p (j r t)"))

            def tanh(j):
                nc.scalar.activation(out=v[:, j], in_=a_sb[:, j], func=ACT.Tanh)

            def tanh_sq(j):
                nc.scalar.activation(out=v[:, j], in_=v[:, j], func=ACT.Square, scale=col(root, 2 * PLANES + j))

            def back(j):
                banks = []
                cs = slice(j * P, (j + 1) * P)
                for hb in range(2):
                    bank = psum.tile([P, 512], F32, name="bank")
                    nc.tensor.matmul_mx(
                        out=bank[:],
                        lhsT=g_codes[:, cs].bitcast(FP8X4),
                        lhsT_scale=g_scales[:, cs],
                        rhs=w_sb[:, 2 * hb * HB : 2 * (hb + 1) * HB].bitcast(FP4X4),
                        rhs_scale=w_scl[:, hb * HB : (hb + 1) * HB],
                        start=True,
                        stop=True,
                    )
                    banks.append(bank)
                return banks

            def v_mul(j, banks):
                for hb in range(2):
                    hs = slice(hb * HB, (hb + 1) * HB)
                    nc.vector.scalar_tensor_tensor(
                        out=v[:, j, hs], in0=v[:, j, hs], scalar=col(sq_in, 2 * PLANES + j), in1=banks[hb][:], op0=ALU.subtract, op1=ALU.mult
                    )

            def d2_square(j):
                nc.scalar.activation(out=d2_pl[:, j], in_=v[:, j], func=ACT.Square, scale=col(root, PLANES + j))

            def x2_square(j, d0, d1):
                nc.scalar.activation(out=x2_pl[:, j, d0:d1], in_=x_sb[:, j, d0:d1], func=ACT.Square, scale=col(root, j))

            def x2_vector(j, d0, d1):
                nc.vector.scalar_tensor_tensor(
                    out=x2_pl[:, j, d0:d1], in0=x_sb[:, j, d0:d1], scalar=col(sq_in, j), in1=x_sb[:, j, d0:d1], op0=ALU.mult, op1=ALU.mult
                )

            def interleave(dst, src):
                nc.vector.tensor_copy(out=dst.rearrange("p (c i) t -> p c t i", i=4), in_=src.rearrange("p t (c i) -> p c t i", i=4))

            def d_int_pool(g, hb):
                dst = work.tile([P, HB, T], BF16, align_bytes=64, name="d2_int", bufs=2)
                for n0 in (0, 256):
                    nc.gpsimd.tensor_scalar(
                        out=dst[:, n0 : n0 + 256],
                        in0=d2_pl[:, T * g : T * (g + 1), hb * HB + n0 : hb * HB + n0 + 256].rearrange("p t n -> p n t"),
                        scalar1=1.0,
                        scalar2=0.0,
                        op0=ALU.mult,
                        op1=ALU.add,
                    )
                ints["d2", g, hb] = dst

            def d_int(src, g, hb, name):
                dst = work.tile([P, HB, T], BF16, align_bytes=64, name=name, bufs=2)
                interleave(dst[:], src[:, T * g : T * (g + 1), hb * HB : (hb + 1) * HB])
                return dst

            def d_quant(src, g, hb, codes, scales):
                hs = slice(hb * HB, (hb + 1) * HB)
                nc.vector.quantize_mx(out=codes[:, g, hs].bitcast(FP8X4), scales=scales[:, g, hs], in_=src[:].rearrange("p n t -> p (n t)"))

            def x_turn(c, g):
                bank = psum.tile([P, 512], F32, name="bank")
                for i in range(2):
                    d0 = c * W + i * P
                    nc.tensor.matmul(
                        bank[:].bitcast(BF16)[:, i * 512 : (i + 1) * 512].rearrange("p (n t) -> p n t", t=T),
                        lhsT=ident_bf[:],
                        rhs=x_sb[:, T * g : T * (g + 1), d0 : d0 + P].rearrange("p t n -> p n t"),
                        start=True,
                        stop=True,
                    )
                return bank

            def xp_mul(bank, g, dst):
                nc.vector.tensor_tensor(
                    out=dst[:, g],
                    in0=bank[:].bitcast(BF16).rearrange("p (n t) -> p n t", t=T),
                    in1=p_sb[:, T * g : T * (g + 1)].unsqueeze(1).to_broadcast([P, W, T]),
                    op=ALU.mult,
                )

            def x_quant(src, name):
                codes = work.tile([P, G * W], U32, align_bytes=64, name=name + "_codes", bufs=3)
                scales = work.tile([P, G * W], U8, align_bytes=64, name=name + "_scales", bufs=3)
                nc.vector.quantize_mx(out=codes[:].bitcast(FP8X4), scales=scales[:], in_=src[:].rearrange("p g n t -> p (g n t)"))
                return codes, scales

            def product_pass(bank, lhs, m, rhs_codes, rhs_scales, hb, g):
                codes, scales = lhs
                c0 = g * W + m * P
                nc.tensor.matmul_mx(
                    out=bank[:],
                    lhsT=codes[:, c0 : c0 + P].bitcast(FP8X4),
                    lhsT_scale=scales[:, c0 : c0 + P],
                    rhs=rhs_codes[:, g, hb * HB : (hb + 1) * HB].bitcast(FP8X4),
                    rhs_scale=rhs_scales[:, g, hb * HB : (hb + 1) * HB],
                    start=(g == 0),
                    stop=(g == G - 1),
                )

            def ars(fb):
                r = epi.tile([P, HB], F32, name="r")
                nc.scalar.activation(out=r[:], in_=fb[:], func=ACT.Abs_reciprocal_sqrt, scale=1.0 / N, bias=DAMP)
                return r

            def square_r(r):
                r2 = epi.tile([P, HB], F32, name="r2")
                nc.scalar.activation(out=r2[:], in_=r[:], func=ACT.Square)
                return r2

            def square_r_pool(r):
                r2 = epi.tile([P, HB], F32, name="r2")
                nc.gpsimd.tensor_tensor(out=r2[:], in0=r[:], in1=r[:], op=ALU.mult)
                return r2

            def grad_times(gb, r):
                y = epi.tile([P, HB], F32, name="y", bufs=8)
                nc.vector.scalar_tensor_tensor(out=y[:], in0=gb[:], scalar=-1.0 / 32.0, in1=r[:], op0=ALU.mult, op1=ALU.mult)
                return y

            def store(y, d0, hb):
                nc.sync.dma_start(out=out[d0 : d0 + P, hb * HB : (hb + 1) * HB], in_=y[:])

            nc.scalar.activation(out=s_abs[:], in_=s_sb[:], func=ACT.Abs)
            qs = slice(2 * PLANES, 3 * PLANES)
            nc.vector.tensor_scalar(out=sq_in[:, qs], in0=q_sb[:], scalar1=1e-30, scalar2=None, op0=ALU.max)
            nc.vector.reciprocal(out=q_inv[:], in_=sq_in[:, qs])
            nc.vector.tensor_tensor(out=sq_in[:, PLANES : 2 * PLANES], in0=q_inv[:], in1=s_abs[:], op=ALU.mult)

            def take_root(c0, c1):
                nc.gpsimd.tensor_tensor(out=root[:, c0:c1], in0=sq_in[:, c0:c1], in1=half[:, c0:c1], op=ALU.pow)

            take_root(PLANES, 3 * PLANES)
            nc.gpsimd.tensor_copy(out=ident_bf[:], in_=ident[:])

            def scalar_interleave(dst, g, hb, n0):
                nc.scalar.copy(
                    out=dst[:, n0 : n0 + 256].rearrange("p (c i) t -> p c t i", i=4),
                    in_=d2_pl[:, T * g : T * (g + 1), hb * HB + n0 : hb * HB + n0 + 256].rearrange("p t (c i) -> p c t i", i=4),
                )

            def d_step(kind, g, hb):
                src, codes, scales = (v, dq_codes, dq_scales) if kind == "dq" else (d2_pl, d2_codes, d2_scales)
                if (kind, g, hb) not in ints:
                    ints[kind, g, hb] = d_int(src, g, hb, kind + "_int")
                else:
                    d_quant(ints[kind, g, hb], g, hb, codes, scales)

            ints = {}
            xp_int = {}

            def xp(c, g):
                if c not in xp_int:
                    dst = work.tile([P, G, W, T], BF16, align_bytes=64, name="xp_int", bufs=N_CHUNKS)
                    xp_int[c] = dst
                xp_mul(x_turn(c, g), g, xp_int[c])

            widen(0, 2)
            b0 = g_turn(0)
            widen(2, 2)
            b1 = g_turn(2)
            tanh(0)
            tanh(1)
            g_mul(b0, 0, 0)
            g_mul(b0, 1, 1)
            tanh_sq(0)
            g_mul(b1, 0, 2)
            g_quant(0, 2)
            g_mul(b1, 1, 3)
            banks = back(0)
            g_quant(2, 2)
            for j in range(PLANES):
                if j + 2 < PLANES:
                    tanh(j + 2)
                if j > 0:
                    d2_square(j - 1)
                if j + 1 < PLANES:
                    tanh_sq(j + 1)
                v_mul(j, banks)
                if j + 1 < PLANES:
                    banks = back(j + 1)
                if j == 0:
                    widen(4, 2)
                    b0 = g_turn(4)
                    widen(6, 2)
                    b1 = g_turn(6)
                if j == 1:
                    g_mul(b0, 0, 4)
                    g_mul(b0, 1, 5)
                    g_mul(b1, 0, 6)
                if j == 2:
                    g_quant(4, 2)
                    g_mul(b1, 1, 7)
                    xp(0, 0)
                    g_quant(6, 2)
                    xp(1, 0)
                if j == 3:
                    nc.vector.tensor_tensor(out=sq_in[:, 0:PLANES], in0=p_sb[:], in1=s_abs[:], op=ALU.mult)
                    take_root(0, PLANES)
                    d_step("dq", 0, 0)
                    d_step("dq", 0, 1)
                if j == 4:
                    d_int_pool(0, 0)
                    d_int_pool(0, 1)
                    xp(0, 1)
                    xp(1, 1)
                    xp(2, 0)
                if j == 5:
                    xp(2, 1)
                    xp(3, 0)
                if j == 6:
                    d_step("dq", 0, 0)
                    d_step("dq", 0, 1)
                if j == 7:
                    d_step("d2", 0, 0)
                    xp(3, 1)
                    d_step("d2", 0, 1)
            x2_square(0, 0, 2 * W)
            d2_square(PLANES - 1)
            d_step("dq", 1, 0)
            d_step("dq", 1, 1)
            d_step("d2", 1, 0)
            for j in range(1, PLANES):
                x2_square(j, 0, 2 * W)
            dst = work.tile([P, HB, T], BF16, align_bytes=64, name="d2_int", bufs=2)
            ints["d2", 1, 1] = dst
            scalar_interleave(dst, 1, 1, 256)

            x2_int, x2_q, xp_q = {}, {}, {}

            def x2(c, g):
                if c not in x2_int:
                    dst = work.tile([P, G, W, T], BF16, align_bytes=64, name="x2_int")
                    x2_int[c] = dst
                interleave(x2_int[c][:, g], x2_pl[:, T * g : T * (g + 1), c * W : (c + 1) * W])

            def quant_x2(c):
                x2_q[c] = x_quant(x2_int[c], "x2")

            def quant_xp(c):
                xp_q[c] = x_quant(xp_int[c], "xp")

            x2(0, 0)
            interleave(ints["d2", 1, 1][:, 0:256], d2_pl[:, T:PLANES, HB : HB + 256])
            x2(0, 1)
            quant_x2(0)
            quant_xp(0)

            BLOCKS = [(m, hb) for m in range(W // P) for hb in range(2)]
            fisher, grad, roots = {}, {}, {}

            def products(c, k, passes=((0, 1),)):
                for group in passes:
                    for made, lhs, codes, scales in ((fisher, x2_q, d2_codes, d2_scales), (grad, xp_q, dq_codes, dq_scales)):
                        for m, hb in BLOCKS[k : k + 2]:
                            if group[0] == 0:
                                bank = psum.tile([P, 512], F32, name="bank")
                                made[c, m, hb] = bank
                            for g in group:
                                product_pass(made[c, m, hb], lhs[c], m, codes, scales, hb, g)

            for k in (0, 2):
                products(0, k, ((0,),))
            d_step("d2", 1, 0)
            d_step("d2", 1, 1)
            d_step("dq", 1, 0)
            d_step("dq", 1, 1)
            for k in (0, 2):
                products(0, k, ((1,),))
            for j in range(PLANES - 2):
                x2_square(j, 2 * W, D)
            nc.scalar.activation(out=warm[:], in_=warm[:], func=ACT.Abs_reciprocal_sqrt, bias=1.0)
            x2(1, 0)
            x2(1, 1)
            quant_xp(1)
            quant_x2(1)
            order = [(c, m, hb) for c in range(N_CHUNKS) for m, hb in BLOCKS]
            roots[order[0]] = ars(fisher[order[0]])
            for b, key in enumerate(order):
                c, m, hb = key
                k = b % len(BLOCKS)
                nx = c + 1
                if c == 0 and k < 2:
                    x2_square(PLANES - 2 + k, 2 * W, D)
                if c + 2 < N_CHUNKS:
                    if k == 1:
                        x2(c + 2, 0)
                    if k == 2:
                        x2(c + 2, 1)
                        quant_xp(c + 2)
                    if k == 3:
                        quant_x2(c + 2)
                if k == 2 and nx < N_CHUNKS:
                    products(nx, 0)
                if b + 1 < len(order):
                    roots[order[b + 1]] = ars(fisher[order[b + 1]])
                r = roots[key]
                y = grad_times(grad[key], (square_r_pool if b in (1, 9, 11, 13) else square_r)(r))
                store(y, c * W + m * P, hb)
                if k == 3 and nx < N_CHUNKS:
                    products(nx, 2)
